import numpy as np
import ml_dtypes

BF16 = ml_dtypes.bfloat16


def bf(x):
    return np.asarray(x, np.float32).astype(BF16)


def f32(x):
    return np.asarray(x, np.float32)


def f64(x):
    return np.asarray(x).astype(np.float64)


def striped(idx):
    return np.tile(idx.reshape(-1, 16).T, (8, 1))


def rows(idx, k):
    return np.tile(idx, (k, 1))


def look(tab, idx):
    return np.take_along_axis(f64(tab), rows(idx, len(tab)), axis=1)


K, S, V, N = 256, 2048, 2048, 2048


def setup_inputs():
    return {"tab": f32(np.random.standard_normal((2, K, S))), "y": f32(np.random.standard_normal((K, V))), "offs": striped(np.random.permutation(S)[:N])}


def reference(tab, y, offs):
    idx = offs[:16].T.reshape(-1)
    x = (look(tab[0], idx) - f64(y)) * (np.maximum(look(tab[1], idx), 0.0))
    return x

@@ -1,0 +1,57 @@
+import concourse.mybir as mybir
+
+F32 = mybir.dt.float32
+U16 = mybir.dt.uint16
+SUBTRACT = mybir.AluOpType.subtract
+MULT = mybir.AluOpType.mult
+RELU = mybir.ActivationFunctionType.Relu
+
+P = 128
+STRIPE = 16
+PIECE = 512
+
+FLOPS = 3 * 256 * 2048
+
+
+def tile_lookup_vg_subrelu_out_kernel(tc, tab, y, offs, out):
+    nc = tc.nc
+    rows, n = out.shape
+    places = tab.shape[2]
+    blocks = rows // P
+    pieces = n // PIECE
+
+    with (
+        tc.tile_pool(name="lists", bufs=1) as lists,
+        tc.tile_pool(name="loads", bufs=1) as loads,
+        tc.tile_pool(name="work", bufs=4) as work,
+    ):
+        offsets = lists.tile([P, n // STRIPE], U16, name="offsets")
+        nc.sync.dma_start(offsets[:], offs)
+
+        gates, values, streams = [], [], []
+        for b in range(blocks):
+            r = slice(b * P, (b + 1) * P)
+            gate_table = loads.tile([P, places], F32, name=f"gate_table{b}")
+            value_table = loads.tile([P, places], F32, name=f"value_table{b}")
+            stream = loads.tile([P, n], F32, name=f"stream{b}")
+            nc.sync.dma_start(gate_table[:], tab[1, r, :])
+            nc.sync.dma_start(value_table[:], tab[0, r, :])
+            for p in range(pieces):
+                j = slice(p * PIECE, (p + 1) * PIECE)
+                nc.sync.dma_start(stream[:, j], y[r, j])
+            gates.append(gate_table)
+            values.append(value_table)
+            streams.append(stream)
+
+        for b in range(blocks):
+            r = slice(b * P, (b + 1) * P)
+            for p in range(pieces):
+                j = slice(p * PIECE, (p + 1) * PIECE)
+                entries = offsets[:, p * PIECE // STRIPE : (p + 1) * PIECE // STRIPE]
+                gate = work.tile([P, PIECE], F32, name="gate")
+                nc.scalar.activation(gate[:], gates[b][:].indirect(entries), RELU)
+                diff = work.tile([P, PIECE], F32, name="diff")
+                nc.vector.tensor_tensor(diff[:], values[b][:].indirect(entries), streams[b][:, j], SUBTRACT)
+                x = work.tile([P, PIECE], F32, name="x")
+                nc.vector.tensor_tensor(x[:], diff[:], gate[:], MULT)
+                nc.sync.dma_start(out[r, j], x[:])

@@ -9,6 +9,7 @@ RELU = mybir.ActivationFunctionType.Relu
 P = 128
 STRIPE = 16
 PIECE = 512
+LEAD = 2
 
 FLOPS = 3 * 256 * 2048
 
@@ -31,27 +32,34 @@ def tile_lookup_vg_subrelu_out_kernel(tc, tab, y, offs, out):
         gates, values, streams = [], [], []
         for b in range(blocks):
             r = slice(b * P, (b + 1) * P)
-            gate_table = loads.tile([P, places], F32, name=f"gate_table{b}")
             value_table = loads.tile([P, places], F32, name=f"value_table{b}")
+            gate_table = loads.tile([P, places], F32, name=f"gate_table{b}")
             stream = loads.tile([P, n], F32, name=f"stream{b}")
-            nc.sync.dma_start(gate_table[:], tab[1, r, :])
             nc.sync.dma_start(value_table[:], tab[0, r, :])
             for p in range(pieces):
+                if p == LEAD:
+                    nc.sync.dma_start(gate_table[:], tab[1, r, :])
                 j = slice(p * PIECE, (p + 1) * PIECE)
                 nc.sync.dma_start(stream[:, j], y[r, j])
-            gates.append(gate_table)
             values.append(value_table)
+            gates.append(gate_table)
             streams.append(stream)
 
-        for b in range(blocks):
-            r = slice(b * P, (b + 1) * P)
-            for p in range(pieces):
+        steps = [(b, p) for b in range(blocks) for p in range(pieces)]
+        diffs, opened = [], []
+        for i in range(len(steps) + LEAD):
+            if i < len(steps):
+                b, p = steps[i]
                 j = slice(p * PIECE, (p + 1) * PIECE)
                 entries = offsets[:, p * PIECE // STRIPE : (p + 1) * PIECE // STRIPE]
                 gate = work.tile([P, PIECE], F32, name="gate")
                 nc.scalar.activation(gate[:], gates[b][:].indirect(entries), RELU)
                 diff = work.tile([P, PIECE], F32, name="diff")
                 nc.vector.tensor_tensor(diff[:], values[b][:].indirect(entries), streams[b][:, j], SUBTRACT)
+                diffs.append(diff)
+                opened.append(gate)
+            if i >= LEAD:
+                b, p = steps[i - LEAD]
                 x = work.tile([P, PIECE], F32, name="x")
-                nc.vector.tensor_tensor(x[:], diff[:], gate[:], MULT)
-                nc.sync.dma_start(out[r, j], x[:])
+                nc.vector.tensor_tensor(x[:], diffs[i - LEAD][:], opened[i - LEAD][:], MULT)
+                nc.sync.dma_start(out[b * P : (b + 1) * P, p * PIECE : (p + 1) * PIECE], x[:])

@@ -18,48 +18,49 @@ def tile_lookup_vg_subrelu_out_kernel(tc, tab, y, offs, out):
     nc = tc.nc
     rows, n = out.shape
     places = tab.shape[2]
-    blocks = rows // P
-    pieces = n // PIECE
+    steps = [(b, slice(a, a + PIECE)) for b in range(rows // P) for a in range(0, n, PIECE)]
 
     with (
         tc.tile_pool(name="lists", bufs=1) as lists,
         tc.tile_pool(name="loads", bufs=1) as loads,
-        tc.tile_pool(name="work", bufs=4) as work,
+        tc.tile_pool(name="work", bufs=len(steps)) as work,
     ):
+        zero = loads.tile([P, 1], F32, name="zero")
+        nc.gpsimd.memset(zero[:], 0.0)
+        warmed = loads.tile([P, 1], F32, name="warmed")
+        nc.scalar.activation(warmed[:], zero[:], RELU)
+
         offsets = lists.tile([P, n // STRIPE], U16, name="offsets")
         nc.sync.dma_start(offsets[:], offs)
 
         gates, values, streams = [], [], []
-        for b in range(blocks):
-            r = slice(b * P, (b + 1) * P)
-            value_table = loads.tile([P, places], F32, name=f"value_table{b}")
-            gate_table = loads.tile([P, places], F32, name=f"gate_table{b}")
-            stream = loads.tile([P, n], F32, name=f"stream{b}")
-            nc.sync.dma_start(value_table[:], tab[0, r, :])
-            for p in range(pieces):
-                if p == LEAD:
-                    nc.sync.dma_start(gate_table[:], tab[1, r, :])
-                j = slice(p * PIECE, (p + 1) * PIECE)
-                nc.sync.dma_start(stream[:, j], y[r, j])
-            values.append(value_table)
-            gates.append(gate_table)
+        for b, j in steps:
+            rows_b = slice(b * P, (b + 1) * P)
+            if j.start == 0:
+                value_table = loads.tile([P, places], F32, name=f"value_table{b}")
+                nc.sync.dma_start(value_table[:], tab[0, rows_b, :])
+                values.append(value_table)
+            if j.start == LEAD * PIECE:
+                gate_table = loads.tile([P, places], F32, name=f"gate_table{b}")
+                nc.sync.dma_start(gate_table[:], tab[1, rows_b, :])
+                gates.append(gate_table)
+            stream = loads.tile([P, PIECE], F32, name=f"stream{b}_{j.start}")
+            nc.sync.dma_start(stream[:], y[rows_b, j])
             streams.append(stream)
 
-        steps = [(b, p) for b in range(blocks) for p in range(pieces)]
         diffs, opened = [], []
         for i in range(len(steps) + LEAD):
             if i < len(steps):
-                b, p = steps[i]
-                j = slice(p * PIECE, (p + 1) * PIECE)
-                entries = offsets[:, p * PIECE // STRIPE : (p + 1) * PIECE // STRIPE]
+                b, j = steps[i]
+                entries = offsets[:, j.start // STRIPE : j.stop // STRIPE]
                 gate = work.tile([P, PIECE], F32, name="gate")
                 nc.scalar.activation(gate[:], gates[b][:].indirect(entries), RELU)
-                diff = work.tile([P, PIECE], F32, name="diff")
-                nc.vector.tensor_tensor(diff[:], values[b][:].indirect(entries), streams[b][:, j], SUBTRACT)
-                diffs.append(diff)
                 opened.append(gate)
+                diff = work.tile([P, PIECE], F32, name="diff")
+                nc.vector.tensor_tensor(diff[:], values[b][:].indirect(entries), streams[i][:], SUBTRACT)
+                diffs.append(diff)
             if i >= LEAD:
-                b, p = steps[i - LEAD]
-                x = work.tile([P, PIECE], F32, name="x")
+                b, j = steps[i - LEAD]
+                x = streams[i % len(steps)]
                 nc.vector.tensor_tensor(x[:], diffs[i - LEAD][:], opened[i - LEAD][:], MULT)
-                nc.sync.dma_start(out[b * P : (b + 1) * P, p * PIECE : (p + 1) * PIECE], x[:])
+                nc.sync.dma_start(out[b * P : (b + 1) * P, j], x[:])

import concourse.mybir as mybir

F32 = mybir.dt.float32
U16 = mybir.dt.uint16
SUBTRACT = mybir.AluOpType.subtract
MULT = mybir.AluOpType.mult
RELU = mybir.ActivationFunctionType.Relu

P = 128
STRIPE = 16
PIECE = 512
LEAD = 2

FLOPS = 3 * 256 * 2048


def tile_lookup_vg_subrelu_out_kernel(tc, tab, y, offs, out):
    nc = tc.nc
    rows, n = out.shape
    places = tab.shape[2]
    steps = [(b, slice(a, a + PIECE)) for b in range(rows // P) for a in range(0, n, PIECE)]

    with (
        tc.tile_pool(name="lists", bufs=1) as lists,
        tc.tile_pool(name="loads", bufs=1) as loads,
        tc.tile_pool(name="work", bufs=len(steps)) as work,
    ):
        zero = loads.tile([P, 1], F32, name="zero")
        nc.gpsimd.memset(zero[:], 0.0)
        warmed = loads.tile([P, 1], F32, name="warmed")
        nc.scalar.activation(warmed[:], zero[:], RELU)

        offsets = lists.tile([P, n // STRIPE], U16, name="offsets")
        nc.sync.dma_start(offsets[:], offs)

        gates, values, streams = [], [], []
        for b, j in steps:
            rows_b = slice(b * P, (b + 1) * P)
            if j.start == 0:
                value_table = loads.tile([P, places], F32, name=f"value_table{b}")
                nc.sync.dma_start(value_table[:], tab[0, rows_b, :])
                values.append(value_table)
            if j.start == LEAD * PIECE:
                gate_table = loads.tile([P, places], F32, name=f"gate_table{b}")
                nc.sync.dma_start(gate_table[:], tab[1, rows_b, :])
                gates.append(gate_table)
            stream = loads.tile([P, PIECE], F32, name=f"stream{b}_{j.start}")
            nc.sync.dma_start(stream[:], y[rows_b, j])
            streams.append(stream)

        diffs, opened = [], []
        for i in range(len(steps) + LEAD):
            if i < len(steps):
                b, j = steps[i]
                entries = offsets[:, j.start // STRIPE : j.stop // STRIPE]
                gate = work.tile([P, PIECE], F32, name="gate")
                nc.scalar.activation(gate[:], gates[b][:].indirect(entries), RELU)
                opened.append(gate)
                diff = work.tile([P, PIECE], F32, name="diff")
                nc.vector.tensor_tensor(diff[:], values[b][:].indirect(entries), streams[i][:], SUBTRACT)
                diffs.append(diff)
            if i >= LEAD:
                b, j = steps[i - LEAD]
                x = streams[i % len(steps)]
                nc.vector.tensor_tensor(x[:], diffs[i - LEAD][:], opened[i - LEAD][:], MULT)
                nc.sync.dma_start(out[b * P : (b + 1) * P, j], x[:])
